import numpy as np
import ml_dtypes


def mxq(x, axis, fmt="e4m3"):
    dtype, down = {"e4m3": (ml_dtypes.float8_e4m3fn, 7), "e5m2": (ml_dtypes.float8_e5m2, 14)}[fmt]
    v = np.moveaxis(np.asarray(x, np.float32).astype(ml_dtypes.bfloat16).astype(np.float64), axis, -1)
    blocks = v.reshape(v.shape[:-1] + (-1, 32))
    amax = np.abs(blocks).max(-1, keepdims=True)
    byte = np.maximum(np.where(amax > 0, np.frexp(amax)[1] - 1 + 127, 0) - down, 1)
    scale = np.exp2(byte - 127.0)
    codes = (blocks / scale).astype(np.float32).astype(dtype).astype(np.float64)
    return np.moveaxis((codes * scale).reshape(v.shape), -1, axis)


WIDE = False


def mx_kscale(k):
    if not WIDE:
        return np.ones(k)
    levels = np.array([30, -30])
    if k % 512:
        return np.exp2(np.random.permutation(np.resize(levels, k // 32))).repeat(32)
    a = np.empty((k // 512, 16))
    for p in range(k // 512):
        a[p, :8] = np.random.permutation(np.resize(levels, 8))
        for g in range(8):
            far = levels[np.abs(levels - a[p, g]) >= 10]
            a[p, g + 8] = far[np.random.randint(len(far))]
    return np.exp2(a.ravel()).repeat(32)


def f64(x):
    return np.asarray(x).astype(np.float64)


def striped(idx):
    return np.tile(np.asarray(idx).reshape(-1, 16).T, (8, 1)).astype(np.uint16)


def unstriped(offs):
    return offs[:16].T.reshape(-1).astype(np.int64)


E2M1 = np.array([0.0, 0.5, 1.0, 1.5, 2.0, 3.0, 4.0, 6.0, -0.0, -0.5, -1.0, -1.5, -2.0, -3.0, -4.0, -6.0])


def pack_weight(w, fmt):
    k, n = w.shape
    w = f64(np.asarray(w, np.float32).astype(ml_dtypes.bfloat16)).reshape(k // 32, 32, n)
    amax = np.abs(w).max(1)
    if fmt in ("e4m3", "e5m2"):
        byte = np.frexp(amax)[1] - 1 + 127 - (7 if fmt == "e4m3" else 14)
    else:
        mant, ex = np.frexp(amax / 6.0)
        byte = np.where(mant > 0.5, ex, ex - 1) + 127
    byte = np.clip(np.where(amax > 0, byte, 1), 1, 254)
    scaled = (w * np.exp2(127.0 - byte)[:, None, :]).reshape(k, n).astype(np.float32)
    by_word = np.ascontiguousarray(scaled.reshape(k // 512, 128, 4, n).transpose(0, 1, 3, 2))
    if fmt in ("e4m3", "e5m2"):
        words = by_word.astype(ml_dtypes.float8_e4m3fn if fmt == "e4m3" else ml_dtypes.float8_e5m2).view(np.uint8)
    else:
        c = by_word.astype(ml_dtypes.float4_e2m1fn).view(np.uint8) & 0xF
        words = (c[..., 0::2] | (c[..., 1::2] << 4)).reshape(k // 512, 128, 2 * n)
    return np.ascontiguousarray(words), np.ascontiguousarray(byte.astype(np.uint8).reshape(k // 512, 16, n))


def unpack_weight(words, scales, fmt):
    g, _, n = scales.shape
    words = np.ascontiguousarray(words).reshape(g, 128, n, -1)
    if fmt in ("e4m3", "e5m2"):
        vals = words.view(ml_dtypes.float8_e4m3fn if fmt == "e4m3" else ml_dtypes.float8_e5m2).astype(np.float64)
    else:
        nib = np.empty((g, 128, n, 4), np.uint8)
        nib[..., 0::2] = words & 0xF
        nib[..., 1::2] = words >> 4
        vals = E2M1[nib]
    vals = vals * np.repeat(np.exp2(scales.astype(np.float64) - 127.0), 8, axis=1)[..., None]
    return vals.transpose(0, 1, 3, 2).reshape(g * 512, n)


K, T, J, R, V, I, O, N, S, E = 512, 1024, 256, 512, 1024, 256, 128, 256, 1024, 1024


def setup_inputs():
    n = np.random.standard_normal
    idx = np.random.permutation(V)[:R]
    idx2 = np.random.permutation(T)[:J]
    idx3 = np.random.permutation(J)[:I]
    idx4 = np.random.permutation(I)[:O]
    idx5 = np.random.permutation(J)[:O]
    idx6 = np.random.permutation(S)[:N]
    idx7 = np.random.permutation(E)[:O]
    fk = mx_kscale(K)
    fr = mx_kscale(R)
    tr = np.ones(V)
    tr[idx] = fr
    xtp = pack_weight(n((K, T)) / fk[:, None], "e2m1")
    wtp = pack_weight(n((K, V)) * 1 / np.sqrt(K) * fk[:, None] * tr, "e4m3")
    w2p = pack_weight(n((K, R)) * 1 / np.sqrt(K) * fk[:, None], "e5m2")
    vsp = pack_weight(n((R, S)) * 1 / np.sqrt(R) / fr[:, None], "e2m1")
    return {
        "xt_words": xtp[0],
        "xt_scales": xtp[1],
        "wt_words": wtp[0],
        "wt_scales": wtp[1],
        "w2_words": w2p[0],
        "w2_scales": w2p[1],
        "vs_words": vsp[0],
        "vs_scales": vsp[1],
        "offs": striped(idx),
        "offs2": striped(idx2),
        "offs3": striped(idx3),
        "offs4": striped(idx4),
        "offs5": striped(idx5),
        "offs6": striped(idx6),
        "offs7": striped(idx7),
    }


def reference(xt_words, xt_scales, wt_words, wt_scales, w2_words, w2_scales, vs_words, vs_scales, offs, offs2, offs3, offs4, offs5, offs6, offs7):
    idx = unstriped(offs)
    idx2 = unstriped(offs2)
    idx3 = unstriped(offs3)
    idx4 = unstriped(offs4)
    idx5 = unstriped(offs5)
    idx6 = unstriped(offs6)
    idx7 = unstriped(offs7)
    xtu = unpack_weight(xt_words, xt_scales, "e2m1")
    wtu = unpack_weight(wt_words, wt_scales, "e4m3")
    w2u = unpack_weight(w2_words, w2_scales, "e5m2")
    vsu = unpack_weight(vs_words, vs_scales, "e2m1")
    wtidxg = wtu[:, idx]
    xtidx2g = xtu[:, idx2]
    a = wtidxg.T @ xtidx2g
    b = w2u.T @ xtidx2g
    lb = b[:, 0:1]
    lb2 = b[:, 128:129]
    la = a[:, 0:1]
    h1 = a[:, idx3] * lb
    hid = np.maximum(h1[:, idx4] * lb2, b[:, idx5] * la)
    vsidx6g = vsu[:, idx6]
    hidq = mxq(hid, 0, "e5m2")
    p = vsidx6g.T @ hidq
    y = np.zeros((N, E))
    y[:, idx7] = p
    return y

@@ -1,0 +1,151 @@
+from contextlib import ExitStack
+
+import concourse.mybir as mybir
+
+K, T, J, R, V, I, O, N, S, E = 512, 1024, 256, 512, 1024, 256, 128, 256, 1024, 1024
+FLOPS = 2 * K * R * J * 2 + 2 * R * N * O
+
+P = 128
+PACK = 4
+F32 = mybir.dt.float32
+BF16 = mybir.dt.bfloat16
+I32 = mybir.dt.int32
+U32 = mybir.dt.uint32
+U16 = mybir.dt.uint16
+U8 = mybir.dt.uint8
+E4M3 = mybir.dt.float8_e4m3fn_x4
+E5M2 = mybir.dt.float8_e5m2_x4
+E2M1 = mybir.dt.float4_e2m1fn_x4
+COPY = mybir.ActivationFunctionType.Copy
+MAX = mybir.AluOpType.max
+
+
+def tile_list_leadthenpick_storeleads_store_scattered_kernel(
+    tc, xt_words, xt_scales, wt_words, wt_scales, w2_words, w2_scales, vs_words, vs_scales,
+    offs, offs2, offs3, offs4, offs5, offs6, offs7, out,
+):
+    nc = tc.nc
+    with ExitStack() as ctx:
+        lists = ctx.enter_context(tc.tile_pool(name="lists", bufs=1))
+        keep = ctx.enter_context(tc.tile_pool(name="keep", bufs=1))
+        psum = ctx.enter_context(tc.psum_pool(name="psum", bufs=1))
+
+        def load_list(src, name):
+            tile = lists.tile([P, src.shape[1]], U16, name=name)
+            nc.sync.dma_start(tile[:], src)
+            return tile
+
+        def load_words(queue, src, dtype, columns, name):
+            tile = keep.tile([P, columns], dtype, name=name, align_bytes=64)
+            queue.dma_start(out=tile[:].bitcast(I32), in_=src.bitcast(I32))
+            return tile
+
+        def load_plane(src, columns, name):
+            tile = keep.tile([P, columns], U8, name=name, align_bytes=64)
+            for q in range(4):
+                rows = src[0, 4 * q : 4 * q + 4, :].bitcast(I32)
+                nc.sync.dma_start(
+                    out=tile[32 * q : 32 * q + 32, :].bitcast(I32),
+                    in_=rows.unsqueeze(0).broadcast_to([8, 4, columns // 4]),
+                )
+            return tile
+
+        def gather(window, offsets, count, dtype, name, dealt):
+            tile = keep.tile([P, count], dtype, name=name, align_bytes=64)
+            target = tile[:].rearrange("p (t q) -> p q t", t=PACK) if dealt else tile[:]
+            nc.vector.tensor_copy(target, window[:].indirect(offsets[:]))
+            return tile
+
+        w2_w = load_words(nc.gpsimd, w2_words[0].rearrange("p n t -> p (n t)"), U32, R, "w2_w")
+        l1 = load_list(offs, "l1")
+        wt_s = load_plane(wt_scales, V, "wt_s")
+        l2 = load_list(offs2, "l2")
+        xt_w = load_words(nc.sync, xt_words[0], U16, T, "xt_w")
+        wt_w = load_words(nc.sync, wt_words[0].rearrange("p n t -> p (n t)"), U32, V, "wt_w")
+        w2_s = load_plane(w2_scales, R, "w2_s")
+        xt_s = load_plane(xt_scales, T, "xt_s")
+        l3 = load_list(offs3, "l3")
+        l5 = load_list(offs5, "l5")
+        l4 = load_list(offs4, "l4")
+        l6 = load_list(offs6, "l6")
+        vs_s = load_plane(vs_scales, S, "vs_s")
+        vs_w = load_words(nc.sync, vs_words[0], U16, S, "vs_w")
+        l7 = load_list(offs7, "l7")
+
+        a = [keep.tile([P, 2 * J], F32, name=f"a{t}") for t in range(PACK)]
+        for t in range(PACK):
+            nc.gpsimd.memset(a[t][:, J:], 0.0)
+        pages = [keep.tile([P, E], F32, name=f"page{h}") for h in range(N // P)]
+        for page in pages:
+            nc.gpsimd.memset(page[:], 0.0)
+
+        wg_s = gather(wt_s, l1, R, U8, "wg_s", True)
+        xg_w = gather(xt_w, l2, J, U16, "xg_w", False)
+        wg_w = gather(wt_w, l1, R, U32, "wg_w", True)
+
+        w2d_w = keep.tile([P, R], U32, name="w2d_w", align_bytes=64)
+        w2d_s = keep.tile([P, R], U8, name="w2d_s", align_bytes=64)
+        nc.scalar.copy(w2d_w[:].rearrange("p (t q) -> p q t", t=PACK), w2_w[:].rearrange("p (q t) -> p q t", t=PACK))
+        nc.vector.tensor_copy(w2d_s[:].rearrange("p (t q) -> p q t", t=PACK), w2_s[:].rearrange("p (q t) -> p q t", t=PACK))
+        xg_s = gather(xt_s, l2, J, U8, "xg_s", False)
+
+        b = [keep.tile([P, J], F32, name=f"b{t}") for t in range(PACK)]
+        for t in range(PACK):
+            cols = slice(t * P, (t + 1) * P)
+            if t == 0:
+                a_sum = psum.tile([P, J], F32, name="a_first")[:]
+                b_sum = psum.tile([P, J], F32, name="b_first")[:]
+            else:
+                both = psum.tile([P, 2, J], F32, name=f"both{t}")
+                a_sum, b_sum = both[:, 0, :], both[:, 1, :]
+            nc.tensor.matmul_mx(
+                out=a_sum, lhsT=wg_w[:, cols].bitcast(E4M3), lhsT_scale=wg_s[:, cols],
+                rhs=xg_w[:].bitcast(E2M1), rhs_scale=xg_s[:], start=True, stop=True,
+            )
+            nc.tensor.matmul_mx(
+                out=b_sum, lhsT=w2d_w[:, cols].bitcast(E5M2), lhsT_scale=w2d_s[:, cols],
+                rhs=xg_w[:].bitcast(E2M1), rhs_scale=xg_s[:], start=True, stop=True,
+            )
+            nc.vector.tensor_copy(a[t][:, :J], a_sum)
+            if t == 0:
+                nc.scalar.copy(b[t][:], b_sum)
+            else:
+                nc.vector.tensor_copy(b[t][:], b_sum)
+
+        vg_s = gather(vs_s, l6, N, U8, "vg_s", False)
+        vg_w = gather(vs_w, l6, N, U16, "vg_w", False)
+
+        hid = keep.tile([P, O, PACK], BF16, name="hid", tag="vs_w", align_bytes=64)
+        for s in range(2):
+            u = keep.tile([P, 2, O], F32, name=f"u{s}")
+            v = keep.tile([P, 2, O], F32, name=f"v{s}")
+            for e in range(2):
+                t = 2 * s + e
+                h1 = keep.tile([P, I], F32, name=f"h1_{t}")
+                nc.scalar.activation(out=h1[:], in_=a[t][:].indirect(l3[:]), func=COPY, scale=b[t][:, 0:1])
+                nc.scalar.activation(out=v[:, e, :], in_=b[t][:].indirect(l5[:]), func=COPY, scale=a[t][:, 0:1])
+                nc.scalar.activation(out=u[:, e, :], in_=h1[:].indirect(l4[:]), func=COPY, scale=b[t][:, 128:129])
+            nc.vector.tensor_tensor(
+                hid[:, :, 2 * s : 2 * s + 2], u[:].rearrange("p e o -> p o e"), v[:].rearrange("p e o -> p o e"), MAX
+            )
+
+        hq_w = keep.tile([P, O], U32, name="hq_w", align_bytes=64)
+        hq_s = keep.tile([P, O], U8, name="hq_s", align_bytes=64)
+        nc.vector.quantize_mx(out=hq_w[:].bitcast(E5M2), scales=hq_s[:], in_=hid[:].rearrange("p o t -> p (o t)"))
+
+        for h in range(N // P):
+            cols = slice(h * P, (h + 1) * P)
+            p_bank = psum.tile([P, O], F32, name=f"p_bank{h}")
+            nc.tensor.matmul_mx(
+                out=p_bank[:], lhsT=vg_w[:, cols].bitcast(E2M1), lhsT_scale=vg_s[:, cols],
+                rhs=hq_w[:].bitcast(E5M2), rhs_scale=hq_s[:], start=True, stop=True,
+            )
+            p = keep.tile([P, O], F32, name=f"p{h}")
+            if h == 0:
+                nc.vector.tensor_copy(p[:], p_bank[:])
+                nc.vector.tensor_copy(pages[h][:].indirect(l7[:]), p[:])
+                nc.sync.dma_start(out=out[cols, :], in_=pages[h][:])
+            else:
+                nc.scalar.copy(p[:], p_bank[:])
+                nc.scalar.activation(out=pages[h][:].indirect(l7[:]), in_=p[:], func=COPY)
+                nc.scalar.dma_start(out=out[cols, :], in_=pages[h][:])

@@ -28,6 +28,7 @@ def tile_list_leadthenpick_storeleads_store_scattered_kernel(
     with ExitStack() as ctx:
         lists = ctx.enter_context(tc.tile_pool(name="lists", bufs=1))
         keep = ctx.enter_context(tc.tile_pool(name="keep", bufs=1))
+        reused = ctx.enter_context(tc.tile_pool(name="reused", bufs=1))
         psum = ctx.enter_context(tc.psum_pool(name="psum", bufs=1))
 
         def load_list(src, name):
@@ -40,15 +41,16 @@ def tile_list_leadthenpick_storeleads_store_scattered_kernel(
             queue.dma_start(out=tile[:].bitcast(I32), in_=src.bitcast(I32))
             return tile
 
-        def load_plane(src, columns, name):
-            tile = keep.tile([P, columns], U8, name=name, align_bytes=64)
-            for q in range(4):
-                rows = src[0, 4 * q : 4 * q + 4, :].bitcast(I32)
-                nc.sync.dma_start(
-                    out=tile[32 * q : 32 * q + 32, :].bitcast(I32),
-                    in_=rows.unsqueeze(0).broadcast_to([8, 4, columns // 4]),
-                )
+        def zeroed_plane(engine, columns, name):
+            tile = keep.tile([P, columns], U8, name=name, tag=name, align_bytes=64)
+            engine.memset(tile[:].bitcast(I32), 0)
             return tile
+
+        def load_plane(tile, src, queues=(nc.sync,) * 4):
+            for q, queue in enumerate(queues):
+                queue.dma_start(
+                    out=tile[32 * q : 32 * q + 4, :].bitcast(I32), in_=src[0, 4 * q : 4 * q + 4, :].bitcast(I32)
+                )
 
         def gather(window, offsets, count, dtype, name, dealt):
             tile = keep.tile([P, count], dtype, name=name, align_bytes=64)
@@ -56,82 +58,117 @@ def tile_list_leadthenpick_storeleads_store_scattered_kernel(
             nc.vector.tensor_copy(target, window[:].indirect(offsets[:]))
             return tile
 
-        w2_w = load_words(nc.gpsimd, w2_words[0].rearrange("p n t -> p (n t)"), U32, R, "w2_w")
-        l1 = load_list(offs, "l1")
-        wt_s = load_plane(wt_scales, V, "wt_s")
+        wt_s = zeroed_plane(nc.vector, V, "wt_s")
+        w2_s = zeroed_plane(nc.vector, R, "w2_s")
+        xt_s = zeroed_plane(nc.gpsimd, T, "xt_s")
+        vs_s = zeroed_plane(nc.vector, S, "vs_s")
+
         l2 = load_list(offs2, "l2")
         xt_w = load_words(nc.sync, xt_words[0], U16, T, "xt_w")
+        l1 = load_list(offs, "l1")
+        load_plane(wt_s, wt_scales)
         wt_w = load_words(nc.sync, wt_words[0].rearrange("p n t -> p (n t)"), U32, V, "wt_w")
-        w2_s = load_plane(w2_scales, R, "w2_s")
-        xt_s = load_plane(xt_scales, T, "xt_s")
+        load_plane(w2_s, w2_scales)
+        load_plane(xt_s, xt_scales, (nc.sync, nc.sync, nc.sync, nc.gpsimd))
+        w2_w = load_words(nc.gpsimd, w2_words[0].rearrange("p n t -> p (n t)"), U32, R, "w2_w")
         l3 = load_list(offs3, "l3")
         l5 = load_list(offs5, "l5")
         l4 = load_list(offs4, "l4")
         l6 = load_list(offs6, "l6")
-        vs_s = load_plane(vs_scales, S, "vs_s")
-        vs_w = load_words(nc.sync, vs_words[0], U16, S, "vs_w")
+        load_plane(vs_s, vs_scales)
+        vs_w = reused.tile([P, S], U16, name="vs_w", offset=0, align_bytes=64)
+        nc.sync.dma_start(out=vs_w[:].bitcast(I32), in_=vs_words[0].bitcast(I32))
         l7 = load_list(offs7, "l7")
 
         a = [keep.tile([P, 2 * J], F32, name=f"a{t}") for t in range(PACK)]
         for t in range(PACK):
             nc.gpsimd.memset(a[t][:, J:], 0.0)
-        pages = [keep.tile([P, E], F32, name=f"page{h}") for h in range(N // P)]
-        for page in pages:
-            nc.gpsimd.memset(page[:], 0.0)
 
-        wg_s = gather(wt_s, l1, R, U8, "wg_s", True)
         xg_w = gather(xt_w, l2, J, U16, "xg_w", False)
+        wg_s = gather(wt_s, l1, R, U8, "wg_s", True)
         wg_w = gather(wt_w, l1, R, U32, "wg_w", True)
 
-        w2d_w = keep.tile([P, R], U32, name="w2d_w", align_bytes=64)
-        w2d_s = keep.tile([P, R], U8, name="w2d_s", align_bytes=64)
+        w2d_w = keep.tile([P, R], U32, name="w2d_w", tag="w2d_w", align_bytes=64)
         nc.scalar.copy(w2d_w[:].rearrange("p (t q) -> p q t", t=PACK), w2_w[:].rearrange("p (q t) -> p q t", t=PACK))
-        nc.vector.tensor_copy(w2d_s[:].rearrange("p (t q) -> p q t", t=PACK), w2_s[:].rearrange("p (q t) -> p q t", t=PACK))
-        xg_s = gather(xt_s, l2, J, U8, "xg_s", False)
+        w2_s_by_slot = w2_s[:].rearrange("p (q t) -> p q t", t=PACK)
+        first_s = keep.tile([P, P], U8, name="first_s", align_bytes=64)
+        nc.vector.tensor_copy(first_s[:], w2_s_by_slot[:, :, 0])
+        xg_s = keep.tile([P, J], U8, name="xg_s", align_bytes=64)
+        for half in range(2):
+            nc.vector.tensor_copy(xg_s[:, half * P : (half + 1) * P], xt_s[:].indirect(l2[:, half * 8 : (half + 1) * 8]))
+        rest_s = keep.tile([P, PACK - 1, P], U8, name="rest_s", tag="xt_s", align_bytes=64)
+        nc.vector.tensor_copy(rest_s[:].rearrange("p t q -> p q t"), w2_s_by_slot[:, :, 1:])
+        w2d_s = [first_s[:]] + [rest_s[:, t, :] for t in range(PACK - 1)]
 
         b = [keep.tile([P, J], F32, name=f"b{t}") for t in range(PACK)]
+        banks = [psum.tile([P, 2, J], F32, name=f"bank{t}") for t in range(PACK + 1)]
+
+
+        def product(total, words, dtype, scales, slots):
+            nc.tensor.matmul_mx(
+                out=total[:, slots], lhsT=words.bitcast(dtype), lhsT_scale=scales,
+                rhs=xg_w[:, slots].bitcast(E2M1), rhs_scale=xg_s[:, slots], start=True, stop=True,
+            )
+
         for t in range(PACK):
             cols = slice(t * P, (t + 1) * P)
-            if t == 0:
-                a_sum = psum.tile([P, J], F32, name="a_first")[:]
-                b_sum = psum.tile([P, J], F32, name="b_first")[:]
-            else:
-                both = psum.tile([P, 2, J], F32, name=f"both{t}")
-                a_sum, b_sum = both[:, 0, :], both[:, 1, :]
-            nc.tensor.matmul_mx(
-                out=a_sum, lhsT=wg_w[:, cols].bitcast(E4M3), lhsT_scale=wg_s[:, cols],
-                rhs=xg_w[:].bitcast(E2M1), rhs_scale=xg_s[:], start=True, stop=True,
-            )
-            nc.tensor.matmul_mx(
-                out=b_sum, lhsT=w2d_w[:, cols].bitcast(E5M2), lhsT_scale=w2d_s[:, cols],
-                rhs=xg_w[:].bitcast(E2M1), rhs_scale=xg_s[:], start=True, stop=True,
-            )
+            a_sum, b_sum = banks[t][:, 1, :], banks[t + 1][:, 0, :]
+            for slots in [slice(0, P), slice(P, J)] if t == 0 else [slice(0, J)]:
+                product(a_sum, wg_w[:, cols], E4M3, wg_s[:, cols], slots)
+                product(b_sum, w2d_w[:, cols], E5M2, w2d_s[t], slots)
             nc.vector.tensor_copy(a[t][:, :J], a_sum)
             if t == 0:
                 nc.scalar.copy(b[t][:], b_sum)
             else:
                 nc.vector.tensor_copy(b[t][:], b_sum)
 
+        pages = [
+            keep.tile([P, E], F32, name=f"page{h}", tag=tag, align_bytes=64) for h, tag in enumerate(("xt_s", "w2d_w"))
+        ]
+        for page in pages:
+            nc.gpsimd.memset(page[:], 0.0)
+
         vg_s = gather(vs_s, l6, N, U8, "vg_s", False)
         vg_w = gather(vs_w, l6, N, U16, "vg_w", False)
 
-        hid = keep.tile([P, O, PACK], BF16, name="hid", tag="vs_w", align_bytes=64)
-        for s in range(2):
-            u = keep.tile([P, 2, O], F32, name=f"u{s}")
-            v = keep.tile([P, 2, O], F32, name=f"v{s}")
-            for e in range(2):
-                t = 2 * s + e
+        HALF = O // 2
+        halves = [slice(0, HALF), slice(HALF, O)]
+        hid = [
+            reused.tile([P, HALF, PACK], BF16, name=f"hid{h}", offset=h * HALF * PACK * 2, align_bytes=64) for h in range(2)
+        ]
+
+        def look(target, window, offsets, scale):
+            nc.scalar.activation(out=target, in_=window[:].indirect(offsets), func=COPY, scale=scale)
+
+        for first, count in ((0, 2), (2, 1), (3, 1)):
+            v = keep.tile([P, count, O], F32, name=f"v{first}")
+            if first == 3:
+                u = [keep.tile([P, count, HALF], F32, name=f"u{first}_{h}")[:] for h in range(2)]
+            else:
+                whole = keep.tile([P, count, O], F32, name=f"u{first}")
+                u = [whole[:, :, places] for places in halves]
+            for e in range(count):
+                t = first + e
                 h1 = keep.tile([P, I], F32, name=f"h1_{t}")
-                nc.scalar.activation(out=h1[:], in_=a[t][:].indirect(l3[:]), func=COPY, scale=b[t][:, 0:1])
-                nc.scalar.activation(out=v[:, e, :], in_=b[t][:].indirect(l5[:]), func=COPY, scale=a[t][:, 0:1])
-                nc.scalar.activation(out=u[:, e, :], in_=h1[:].indirect(l4[:]), func=COPY, scale=b[t][:, 128:129])
-            nc.vector.tensor_tensor(
-                hid[:, :, 2 * s : 2 * s + 2], u[:].rearrange("p e o -> p o e"), v[:].rearrange("p e o -> p o e"), MAX
-            )
+                look(h1[:], a[t], l3[:], b[t][:, 0:1])
+                look(v[:, e, :], b[t], l5[:], a[t][:, 0:1])
+                if first == 3:
+                    for h in range(2):
+                        look(u[h][:, e, :], h1, l4[:, 4 * h : 4 * h + 4], b[t][:, 128:129])
+                else:
+                    look(whole[:, e, :], h1, l4[:], b[t][:, 128:129])
+            for h, places in enumerate(halves):
+                nc.vector.tensor_tensor(
+                    hid[h][:, :, first : first + count],
+                    u[h].rearrange("p e o -> p o e"), v[:, :, places].rearrange("p e o -> p o e"), MAX,
+                )
 
         hq_w = keep.tile([P, O], U32, name="hq_w", align_bytes=64)
         hq_s = keep.tile([P, O], U8, name="hq_s", align_bytes=64)
-        nc.vector.quantize_mx(out=hq_w[:].bitcast(E5M2), scales=hq_s[:], in_=hid[:].rearrange("p o t -> p (o t)"))
+        for h, places in enumerate(halves):
+            nc.vector.quantize_mx(
+                out=hq_w[:, places].bitcast(E5M2), scales=hq_s[:, places], in_=hid[h][:].rearrange("p o t -> p (o t)")
+            )
 
         for h in range(N // P):
             cols = slice(h * P, (h + 1) * P)

from contextlib import ExitStack

import concourse.mybir as mybir

K, T, J, R, V, I, O, N, S, E = 512, 1024, 256, 512, 1024, 256, 128, 256, 1024, 1024
FLOPS = 2 * K * R * J * 2 + 2 * R * N * O

P = 128
PACK = 4
F32 = mybir.dt.float32
BF16 = mybir.dt.bfloat16
I32 = mybir.dt.int32
U32 = mybir.dt.uint32
U16 = mybir.dt.uint16
U8 = mybir.dt.uint8
E4M3 = mybir.dt.float8_e4m3fn_x4
E5M2 = mybir.dt.float8_e5m2_x4
E2M1 = mybir.dt.float4_e2m1fn_x4
COPY = mybir.ActivationFunctionType.Copy
MAX = mybir.AluOpType.max


def tile_list_leadthenpick_storeleads_store_scattered_kernel(
    tc, xt_words, xt_scales, wt_words, wt_scales, w2_words, w2_scales, vs_words, vs_scales,
    offs, offs2, offs3, offs4, offs5, offs6, offs7, out,
):
    nc = tc.nc
    with ExitStack() as ctx:
        lists = ctx.enter_context(tc.tile_pool(name="lists", bufs=1))
        keep = ctx.enter_context(tc.tile_pool(name="keep", bufs=1))
        reused = ctx.enter_context(tc.tile_pool(name="reused", bufs=1))
        psum = ctx.enter_context(tc.psum_pool(name="psum", bufs=1))

        def load_list(src, name):
            tile = lists.tile([P, src.shape[1]], U16, name=name)
            nc.sync.dma_start(tile[:], src)
            return tile

        def load_words(queue, src, dtype, columns, name):
            tile = keep.tile([P, columns], dtype, name=name, align_bytes=64)
            queue.dma_start(out=tile[:].bitcast(I32), in_=src.bitcast(I32))
            return tile

        def zeroed_plane(engine, columns, name):
            tile = keep.tile([P, columns], U8, name=name, tag=name, align_bytes=64)
            engine.memset(tile[:].bitcast(I32), 0)
            return tile

        def load_plane(tile, src, queues=(nc.sync,) * 4):
            for q, queue in enumerate(queues):
                queue.dma_start(
                    out=tile[32 * q : 32 * q + 4, :].bitcast(I32), in_=src[0, 4 * q : 4 * q + 4, :].bitcast(I32)
                )

        def gather(window, offsets, count, dtype, name, dealt):
            tile = keep.tile([P, count], dtype, name=name, align_bytes=64)
            target = tile[:].rearrange("p (t q) -> p q t", t=PACK) if dealt else tile[:]
            nc.vector.tensor_copy(target, window[:].indirect(offsets[:]))
            return tile

        wt_s = zeroed_plane(nc.vector, V, "wt_s")
        w2_s = zeroed_plane(nc.vector, R, "w2_s")
        xt_s = zeroed_plane(nc.gpsimd, T, "xt_s")
        vs_s = zeroed_plane(nc.vector, S, "vs_s")

        l2 = load_list(offs2, "l2")
        xt_w = load_words(nc.sync, xt_words[0], U16, T, "xt_w")
        l1 = load_list(offs, "l1")
        load_plane(wt_s, wt_scales)
        wt_w = load_words(nc.sync, wt_words[0].rearrange("p n t -> p (n t)"), U32, V, "wt_w")
        load_plane(w2_s, w2_scales)
        load_plane(xt_s, xt_scales, (nc.sync, nc.sync, nc.sync, nc.gpsimd))
        w2_w = load_words(nc.gpsimd, w2_words[0].rearrange("p n t -> p (n t)"), U32, R, "w2_w")
        l3 = load_list(offs3, "l3")
        l5 = load_list(offs5, "l5")
        l4 = load_list(offs4, "l4")
        l6 = load_list(offs6, "l6")
        load_plane(vs_s, vs_scales)
        vs_w = reused.tile([P, S], U16, name="vs_w", offset=0, align_bytes=64)
        nc.sync.dma_start(out=vs_w[:].bitcast(I32), in_=vs_words[0].bitcast(I32))
        l7 = load_list(offs7, "l7")

        a = [keep.tile([P, 2 * J], F32, name=f"a{t}") for t in range(PACK)]
        for t in range(PACK):
            nc.gpsimd.memset(a[t][:, J:], 0.0)

        xg_w = gather(xt_w, l2, J, U16, "xg_w", False)
        wg_s = gather(wt_s, l1, R, U8, "wg_s", True)
        wg_w = gather(wt_w, l1, R, U32, "wg_w", True)

        w2d_w = keep.tile([P, R], U32, name="w2d_w", tag="w2d_w", align_bytes=64)
        nc.scalar.copy(w2d_w[:].rearrange("p (t q) -> p q t", t=PACK), w2_w[:].rearrange("p (q t) -> p q t", t=PACK))
        w2_s_by_slot = w2_s[:].rearrange("p (q t) -> p q t", t=PACK)
        first_s = keep.tile([P, P], U8, name="first_s", align_bytes=64)
        nc.vector.tensor_copy(first_s[:], w2_s_by_slot[:, :, 0])
        xg_s = keep.tile([P, J], U8, name="xg_s", align_bytes=64)
        for half in range(2):
            nc.vector.tensor_copy(xg_s[:, half * P : (half + 1) * P], xt_s[:].indirect(l2[:, half * 8 : (half + 1) * 8]))
        rest_s = keep.tile([P, PACK - 1, P], U8, name="rest_s", tag="xt_s", align_bytes=64)
        nc.vector.tensor_copy(rest_s[:].rearrange("p t q -> p q t"), w2_s_by_slot[:, :, 1:])
        w2d_s = [first_s[:]] + [rest_s[:, t, :] for t in range(PACK - 1)]

        b = [keep.tile([P, J], F32, name=f"b{t}") for t in range(PACK)]
        banks = [psum.tile([P, 2, J], F32, name=f"bank{t}") for t in range(PACK + 1)]


        def product(total, words, dtype, scales, slots):
            nc.tensor.matmul_mx(
                out=total[:, slots], lhsT=words.bitcast(dtype), lhsT_scale=scales,
                rhs=xg_w[:, slots].bitcast(E2M1), rhs_scale=xg_s[:, slots], start=True, stop=True,
            )

        for t in range(PACK):
            cols = slice(t * P, (t + 1) * P)
            a_sum, b_sum = banks[t][:, 1, :], banks[t + 1][:, 0, :]
            for slots in [slice(0, P), slice(P, J)] if t == 0 else [slice(0, J)]:
                product(a_sum, wg_w[:, cols], E4M3, wg_s[:, cols], slots)
                product(b_sum, w2d_w[:, cols], E5M2, w2d_s[t], slots)
            nc.vector.tensor_copy(a[t][:, :J], a_sum)
            if t == 0:
                nc.scalar.copy(b[t][:], b_sum)
            else:
                nc.vector.tensor_copy(b[t][:], b_sum)

        pages = [
            keep.tile([P, E], F32, name=f"page{h}", tag=tag, align_bytes=64) for h, tag in enumerate(("xt_s", "w2d_w"))
        ]
        for page in pages:
            nc.gpsimd.memset(page[:], 0.0)

        vg_s = gather(vs_s, l6, N, U8, "vg_s", False)
        vg_w = gather(vs_w, l6, N, U16, "vg_w", False)

        HALF = O // 2
        halves = [slice(0, HALF), slice(HALF, O)]
        hid = [
            reused.tile([P, HALF, PACK], BF16, name=f"hid{h}", offset=h * HALF * PACK * 2, align_bytes=64) for h in range(2)
        ]

        def look(target, window, offsets, scale):
            nc.scalar.activation(out=target, in_=window[:].indirect(offsets), func=COPY, scale=scale)

        for first, count in ((0, 2), (2, 1), (3, 1)):
            v = keep.tile([P, count, O], F32, name=f"v{first}")
            if first == 3:
                u = [keep.tile([P, count, HALF], F32, name=f"u{first}_{h}")[:] for h in range(2)]
            else:
                whole = keep.tile([P, count, O], F32, name=f"u{first}")
                u = [whole[:, :, places] for places in halves]
            for e in range(count):
                t = first + e
                h1 = keep.tile([P, I], F32, name=f"h1_{t}")
                look(h1[:], a[t], l3[:], b[t][:, 0:1])
                look(v[:, e, :], b[t], l5[:], a[t][:, 0:1])
                if first == 3:
                    for h in range(2):
                        look(u[h][:, e, :], h1, l4[:, 4 * h : 4 * h + 4], b[t][:, 128:129])
                else:
                    look(whole[:, e, :], h1, l4[:], b[t][:, 128:129])
            for h, places in enumerate(halves):
                nc.vector.tensor_tensor(
                    hid[h][:, :, first : first + count],
                    u[h].rearrange("p e o -> p o e"), v[:, :, places].rearrange("p e o -> p o e"), MAX,
                )

        hq_w = keep.tile([P, O], U32, name="hq_w", align_bytes=64)
        hq_s = keep.tile([P, O], U8, name="hq_s", align_bytes=64)
        for h, places in enumerate(halves):
            nc.vector.quantize_mx(
                out=hq_w[:, places].bitcast(E5M2), scales=hq_s[:, places], in_=hid[h][:].rearrange("p o t -> p (o t)")
            )

        for h in range(N // P):
            cols = slice(h * P, (h + 1) * P)
            p_bank = psum.tile([P, O], F32, name=f"p_bank{h}")
            nc.tensor.matmul_mx(
                out=p_bank[:], lhsT=vg_w[:, cols].bitcast(E2M1), lhsT_scale=vg_s[:, cols],
                rhs=hq_w[:].bitcast(E5M2), rhs_scale=hq_s[:], start=True, stop=True,
            )
            p = keep.tile([P, O], F32, name=f"p{h}")
            if h == 0:
                nc.vector.tensor_copy(p[:], p_bank[:])
                nc.vector.tensor_copy(pages[h][:].indirect(l7[:]), p[:])
                nc.sync.dma_start(out=out[cols, :], in_=pages[h][:])
            else:
                nc.scalar.copy(p[:], p_bank[:])
                nc.scalar.activation(out=pages[h][:].indirect(l7[:]), in_=p[:], func=COPY)
                nc.scalar.dma_start(out=out[cols, :], in_=pages[h][:])
